import numpy as np
import ml_dtypes


def mxq(x, axis, fmt="e4m3"):
    dtype, down = {"e4m3": (ml_dtypes.float8_e4m3fn, 7), "e5m2": (ml_dtypes.float8_e5m2, 14)}[fmt]
    v = np.moveaxis(np.asarray(x, np.float32).astype(ml_dtypes.bfloat16).astype(np.float64), axis, -1)
    blocks = v.reshape(v.shape[:-1] + (-1, 32))
    amax = np.abs(blocks).max(-1, keepdims=True)
    byte = np.maximum(np.where(amax > 0, np.frexp(amax)[1] - 1 + 127, 0) - down, 1)
    scale = np.exp2(byte - 127.0)
    codes = (blocks / scale).astype(np.float32).astype(dtype).astype(np.float64)
    return np.moveaxis((codes * scale).reshape(v.shape), -1, axis)


WIDE = False


def mx_kscale(k):
    if not WIDE:
        return np.ones(k)
    levels = np.array([10, -10, 5, -5, 0])
    if k % 512:
        return np.exp2(np.random.permutation(np.resize(levels, k // 32))).repeat(32)
    a = np.empty((k // 512, 16))
    for p in range(k // 512):
        a[p, :8] = np.random.permutation(np.resize(levels, 8))
        for g in range(8):
            far = levels[np.abs(levels - a[p, g]) >= 10]
            a[p, g + 8] = far[np.random.randint(len(far))]
    return np.exp2(a.ravel()).repeat(32)


def f64(x):
    return np.asarray(x).astype(np.float64)


def striped(idx):
    return np.tile(idx.reshape(-1, 16).T, (8, 1)).astype(np.uint16)


def unstriped(offs):
    return offs[:16].T.reshape(-1).astype(np.int64)


def striped8(idx):
    return np.concatenate([x.reshape(-1, 16).T for x in idx]).astype(np.uint16)


def runs(offs, k):
    lists = np.stack([offs[16 * r : 16 * r + 16].T.reshape(-1) for r in range(8)]).astype(np.int64)
    return lists[np.arange(k) % 512 // 64]


def pack_weight(w):
    k, n = w.shape
    w = f64(np.asarray(w, np.float32).astype(ml_dtypes.bfloat16)).reshape(k // 32, 32, n)
    amax = np.abs(w).max(1)
    byte = np.clip(np.where(amax > 0, np.frexp(amax)[1] - 1 + 127 - 7, 1), 1, 254)
    scaled = (w * np.exp2(127.0 - byte)[:, None, :]).reshape(k, n).astype(np.float32)
    words = np.ascontiguousarray(scaled.reshape(k // 512, 128, 4, n).transpose(0, 1, 3, 2)).astype(ml_dtypes.float8_e4m3fn).view(np.uint8)
    return words, np.ascontiguousarray(byte.astype(np.uint8).reshape(k // 512, 16, n))


def unpack_weight(words, scales):
    g, p, n, _ = words.shape
    vals = np.ascontiguousarray(words).view(ml_dtypes.float8_e4m3fn).astype(np.float64) * np.repeat(np.exp2(scales.astype(np.float64) - 127.0), 8, axis=1)[..., None]
    return vals.transpose(0, 1, 3, 2).reshape(g * 512, n)


E2M1 = np.array([0.0, 0.5, 1.0, 1.5, 2.0, 3.0, 4.0, 6.0, -0.0, -0.5, -1.0, -1.5, -2.0, -3.0, -4.0, -6.0])


def pack_fp4(w):
    k, n = w.shape
    w = f64(np.asarray(w, np.float32).astype(ml_dtypes.bfloat16)).reshape(k // 32, 32, n)
    amax = np.abs(w).max(1)
    mant, ex = np.frexp(amax / 6.0)
    byte = np.clip(np.where(amax > 0, np.where(mant > 0.5, ex, ex - 1) + 127, 1), 1, 254)
    scaled = (w * np.exp2(127.0 - byte)[:, None, :]).reshape(k, n).astype(np.float32)
    c = np.ascontiguousarray(scaled.reshape(k // 512, 128, 4, n).transpose(0, 1, 3, 2)).astype(ml_dtypes.float4_e2m1fn).view(np.uint8) & 0xF
    words = (c[..., 0::2] | (c[..., 1::2] << 4)).reshape(k // 512, 128, 2 * n)
    return np.ascontiguousarray(words), np.ascontiguousarray(byte.astype(np.uint8).reshape(k // 512, 16, n))


def unpack_fp4(words, scales):
    g, _, n = scales.shape
    words = np.ascontiguousarray(words).reshape(g, 128, n, 2)
    nib = np.empty((g, 128, n, 4), np.uint8)
    nib[..., 0::2] = words & 0xF
    nib[..., 1::2] = words >> 4
    vals = E2M1[nib] * np.repeat(np.exp2(scales.astype(np.float64) - 127.0), 8, axis=1)[..., None]
    return vals.transpose(0, 1, 3, 2).reshape(g * 512, n)


def planes(y):
    n, m = y.shape
    v = y.astype(np.float32).astype(ml_dtypes.bfloat16).astype(np.float64).reshape(n // 32, 32, m)
    top = np.abs(v).max(1)
    byte = np.clip(np.where(top > 0, np.frexp(top)[1] - 1 + 127 - 7, 1), 1, 254)
    codes = (v * np.exp2(127.0 - byte)[:, None, :]).reshape(n, m).astype(np.float32).astype(ml_dtypes.float8_e4m3fn).view(np.uint8)
    words = codes.reshape(n // 512, 128, 4, m).transpose(0, 1, 3, 2)
    return np.ascontiguousarray(words), np.ascontiguousarray(byte.astype(np.uint8).reshape(n // 512, 16, m))


K, T, S, N, H = 512, 2048, 512, 512, 512


def setup_inputs():
    n = np.random.standard_normal
    s = mx_kscale(K)[:, None]
    u = mx_kscale(H)
    packed_xT = pack_weight(n((K, T)) * s)
    packed_w1 = pack_fp4(n((K, H)) / np.sqrt(K) / s)
    packed_w2 = pack_fp4(n((H, N)) / np.sqrt(2 * H) / u[:, None])
    packed_w3 = pack_fp4(n((K, N)) / np.sqrt(2 * K) / s)
    return {
        "x_words": packed_xT[0],
        "x_scales": packed_xT[1],
        "w1_words": packed_w1[0],
        "w1_scales": packed_w1[1],
        "gn": (np.random.uniform(0.5, 1.5, (H, 1)) * u[:, None]).astype(np.float32),
        "w2_words": packed_w2[0],
        "w2_scales": packed_w2[1],
        "w3_words": packed_w3[0],
        "w3_scales": packed_w3[1],
        "offs": striped(np.random.permutation(T)[:S]),
        "n1": striped8(np.stack([np.random.permutation(S) for _ in range(8)])),
        "n2": striped8(np.stack([np.random.permutation(S) for _ in range(8)])),
        "n3": striped8(np.stack([np.random.permutation(S) for _ in range(8)])),
        "hz": striped8(np.random.randint(0, T, (8, S))),
        "n4": striped8(np.stack([np.random.permutation(S) for _ in range(8)])),
        "n5": striped8(np.stack([np.random.permutation(S) for _ in range(8)])),
        "n6": striped8(np.stack([np.random.permutation(S) for _ in range(8)])),
    }


def reference(x_words, x_scales, w1_words, w1_scales, gn, w2_words, w2_scales, w3_words, w3_scales, offs, n1, n2, n3, hz, n4, n5, n6):
    xq = unpack_weight(x_words, x_scales)[:, unstriped(offs)]
    y = unpack_fp4(w1_words, w1_scales).T @ xq
    z = f64(gn) * (y + y[np.arange(H)[:, None], runs(n1, H)] - (np.maximum(y[np.arange(H)[:, None], runs(n2, H)], y[np.arange(H)[:, None], runs(n3, H)])))
    x_hz = unpack_weight(x_words, x_scales)[np.arange(K)[:, None], runs(hz, K)]
    h = unpack_fp4(w2_words, w2_scales).T @ mxq(z, 0, "e4m3") + unpack_fp4(w3_words, w3_scales).T @ x_hz
    out_0 = 0.75 * (h * (h[np.arange(N)[:, None], runs(n4, N)]) + (h[np.arange(N)[:, None], runs(n5, N)]) * (h[np.arange(N)[:, None], runs(n6, N)]))
    return (out_0,) + planes(out_0)

@@ -1,0 +1,241 @@
+from contextlib import ExitStack
+
+import concourse.mybir as mybir
+
+K, T, S, N, H = 512, 2048, 512, 512, 512
+FLOPS = 2 * S * (K * H + H * N + K * N)
+
+F32 = mybir.dt.float32
+BF16 = mybir.dt.bfloat16
+I32 = mybir.dt.int32
+U32 = mybir.dt.uint32
+U16 = mybir.dt.uint16
+U8 = mybir.dt.uint8
+FP8X4 = mybir.dt.float8_e4m3fn_x4
+FP4X4 = mybir.dt.float4_e2m1fn_x4
+ALU = mybir.AluOpType
+COPY = mybir.ActivationFunctionType.Copy
+
+P = 128
+PACK = 4
+Z_CHUNKS = ((0, 256), (256, 384), (384, 512))
+OUT_CHUNKS = ((0, 256), (256, 384), (384, 512))
+
+
+def tile_picked_mixhtrimdot_none_po_kernel(
+    tc, x_words, x_scales, w1_words, w1_scales, gn, w2_words, w2_scales, w3_words, w3_scales,
+    offs, n1, n2, n3, hz, n4, n5, n6, out_0, out_1, out_2,
+):
+    nc = tc.nc
+    with ExitStack() as ctx:
+        lists = ctx.enter_context(tc.tile_pool(name="lists", bufs=1))
+        sb = ctx.enter_context(tc.tile_pool(name="sb", bufs=1))
+        psum = ctx.enter_context(tc.psum_pool(name="psum", bufs=1))
+
+        def load_list(src, name):
+            tl = lists.tile([P, S // 16], U16, name=name)
+            nc.sync.dma_start(tl[:], src)
+            return tl
+
+        def load_scale_quadrant(queue, tl, src, q):
+            rows = src[0, 4 * q : 4 * q + 4, :].bitcast(I32)
+            queue.dma_start(tl[32 * q : 32 * q + 32, :].bitcast(I32), rows.partition_broadcast(8))
+
+        def entries(lst, lo, hi):
+            return lst[:, lo // 16 : hi // 16]
+
+        def deal_words(raw, name):
+            dealt = sb.tile([P, 2 * H], U8, name=name, align_bytes=64)
+            nc.vector.tensor_copy(
+                dealt[:].bitcast(U16).rearrange("p (t m) -> p t m", t=PACK),
+                raw[:].bitcast(U16).rearrange("p (m t) -> p t m", t=PACK),
+            )
+            return dealt
+
+        def deal_scales(raw, name):
+            dealt = sb.tile([P, H], U8, name=name, align_bytes=64)
+            nc.vector.tensor_copy(
+                dealt[:].rearrange("p (t m) -> p t m", t=PACK),
+                raw[:].rearrange("p (m t) -> p t m", t=PACK),
+            )
+            return dealt
+
+        def mm(acc, wq, ws, t, codes, scales, start, stop):
+            nc.tensor.matmul_mx(
+                out=acc,
+                lhsT=wq[:, 2 * P * t : 2 * P * (t + 1)].bitcast(FP4X4),
+                lhsT_scale=ws[:, P * t : P * (t + 1)],
+                rhs=codes.bitcast(FP8X4),
+                rhs_scale=scales,
+                start=start,
+                stop=stop,
+            )
+
+        def weave(src, name):
+            woven = sb.tile([P, src.shape[2], PACK], BF16, name=name, align_bytes=64)
+            nc.vector.tensor_copy(
+                woven[:].rearrange("p (c i) t -> p c t i", i=4),
+                src[:].rearrange("p t (c i) -> p c t i", i=4),
+            )
+            return woven
+
+        def quantise(woven, codes, scales):
+            nc.vector.quantize_mx(out=codes.bitcast(FP8X4), scales=scales, in_=woven[:].rearrange("p j t -> p (j t)"))
+
+        xw = sb.tile([P, T], I32, name="xw")
+        xs = sb.tile([P, T], U8, name="xs")
+        w_raw = [sb.tile([P, 2 * H], U8, name="wraw%d" % i) for i in range(3)]
+        s_raw = [sb.tile([P, H], U8, name="sraw%d" % i) for i in range(3)]
+        gain = sb.tile([P, PACK], F32, name="gain")
+
+        offs_t = load_list(offs, "offs_t")
+        for q in range(3):
+            load_scale_quadrant(nc.scalar, xs, x_scales, q)
+        load_scale_quadrant(nc.sync, xs, x_scales, 3)
+        nc.sync.dma_start(w_raw[0][:].bitcast(I32), w1_words[0].bitcast(I32))
+        nc.scalar.dma_start(xw[:], x_words[0].rearrange("p c r -> p (c r)").bitcast(I32))
+        for q in range(4):
+            load_scale_quadrant(nc.sync, s_raw[0], w1_scales, q)
+        hz_t = load_list(hz, "hz_t")
+        n2_t = load_list(n2, "n2_t")
+        n3_t = load_list(n3, "n3_t")
+        nc.sync.dma_start(gain[:], gn.rearrange("(p t) o -> p (t o)", t=PACK))
+        n1_t = load_list(n1, "n1_t")
+        for i, (ww, ws) in ((2, (w3_words, w3_scales)), (1, (w2_words, w2_scales))):
+            nc.sync.dma_start(w_raw[i][:].bitcast(I32), ww[0].bitcast(I32))
+            for q in range(4):
+                load_scale_quadrant(nc.sync, s_raw[i], ws, q)
+        n5_t = load_list(n5, "n5_t")
+        n4_t = load_list(n4, "n4_t")
+        n6_t = load_list(n6, "n6_t")
+
+        hz_scales = sb.tile([P, S], U8, name="hz_scales", align_bytes=64)
+        nc.gpsimd.memset(hz_scales[:], 0)
+
+        pick_s = sb.tile([P, S], U8, name="pick_s", align_bytes=64)
+        nc.vector.tensor_copy(pick_s[:], xs[:].indirect(offs_t[:]))
+        w1q = deal_words(w_raw[0], "w1q")
+        w1s = deal_scales(s_raw[0], "w1s")
+        pick_w = sb.tile([P, S], U32, name="pick_w", align_bytes=64)
+        nc.vector.tensor_copy(pick_w[:], xw[:].bitcast(U32).indirect(offs_t[:]))
+
+        y_ps = [psum.tile([P, S], F32, name="y_ps%d" % t, tag="bank%d" % t) for t in range(PACK)]
+        for t in range(PACK):
+            mm(y_ps[t][:], w1q, w1s, t, pick_w[:], pick_s[:], True, True)
+
+        hz_raw = sb.tile([P, S], U8, name="hz_raw")
+        nc.vector.tensor_copy(hz_raw[:], xs[:].indirect(hz_t[:]))
+        for r in range(4):
+            first = r if r < 2 else 16 + r
+            nc.sync.dma_start(hz_scales[r:P:32, :].bitcast(I32), hz_raw[first:P:32, :].bitcast(I32))
+        hz_w = sb.tile([P, S], U32, name="hz_w", align_bytes=64)
+        nc.vector.tensor_copy(hz_w[:], xw[:].bitcast(U32).indirect(hz_t[:]))
+        w3q = deal_words(w_raw[2], "w3q")
+        w3s = deal_scales(s_raw[2], "w3s")
+        w2q = deal_words(w_raw[1], "w2q")
+        w2s = deal_scales(s_raw[1], "w2s")
+
+        y = [sb.tile([P, S], F32, name="y%d" % t) for t in range(PACK)]
+        gy = [sb.tile([P, S], F32, name="gy%d" % t) for t in range(PACK)]
+        h = [sb.tile([P, S], F32, name="h%d" % t) for t in range(PACK)]
+
+        def chunk_tiles(name, chunks):
+            return [sb.tile([P, PACK, hi - lo], F32, name="%s%d" % (name, c)) for c, (lo, hi) in enumerate(chunks)]
+
+        a, b, m, e, z = (chunk_tiles(name, Z_CHUNKS) for name in ("a", "b", "m", "e", "z"))
+        units = [(c, t) for c in range(len(Z_CHUNKS)) for t in (0, 2)]
+        z_bf = {}
+        h_ps = {}
+
+        def z_gather(c, t):
+            lo, hi = Z_CHUNKS[c]
+            nc.vector.tensor_tensor(z[c][:, t, :], gy[t][:].indirect(entries(n1_t, lo, hi)), e[c][:, t, :], ALU.subtract)
+
+        def second_product(c):
+            lo, hi = Z_CHUNKS[c]
+            w = hi - lo
+            z_w = sb.tile([P, w], U32, name="z_w%d" % c, align_bytes=64)
+            z_s = sb.tile([P, w], U8, name="z_s%d" % c, align_bytes=64)
+            quantise(z_bf[c], z_w[:], z_s[:])
+            for t in range(PACK):
+                h_ps[c, t] = psum.tile([P, S], F32, name="h_ps%d_%d" % (c, t), tag="bank%d" % (PACK * ((c + 1) % 2) + t))
+                mm(h_ps[c, t][:, 0:w], w3q, w3s, t, hz_w[:, lo:hi], hz_scales[:, lo:hi], True, False)
+            for t in range(PACK):
+                mm(h_ps[c, t][:, 0:w], w2q, w2s, t, z_w[:], z_s[:], False, True)
+
+        def h_copy(c, t):
+            lo, hi = Z_CHUNKS[c]
+            nc.scalar.activation(h[t][:, lo:hi], h_ps[c, t][:, 0 : hi - lo], COPY)
+
+        for u, (c, t0) in enumerate(units):
+            lo, hi = Z_CHUNKS[c]
+            for t in (t0, t0 + 1):
+                if c == 0:
+                    nc.scalar.activation(y[t][:], y_ps[t][:], COPY)
+                nc.scalar.activation(a[c][:, t, :], y[t][:].indirect(entries(n2_t, lo, hi)), COPY)
+                nc.scalar.activation(b[c][:, t, :], y[t][:].indirect(entries(n3_t, lo, hi)), COPY)
+            for t in (t0, t0 + 1):
+                if c == 0:
+                    nc.scalar.activation(gy[t][:], y_ps[t][:], COPY, scale=gain[:, t : t + 1])
+            nc.vector.tensor_tensor(m[c][:, t0 : t0 + 2, :], a[c][:, t0 : t0 + 2, :], b[c][:, t0 : t0 + 2, :], ALU.max)
+            for d in (0, 1):
+                t = t0 + d
+                if u > 0:
+                    z_gather(units[u - 1][0], units[u - 1][1] + d)
+                nc.vector.scalar_tensor_tensor(e[c][:, t, :], m[c][:, t, :], gain[:, t : t + 1], gy[t][:, lo:hi], ALU.mult, ALU.subtract)
+            if c > 0 and t0 == 0:
+                z_bf[c - 1] = weave(z[c - 1], "z_bf%d" % (c - 1))
+                second_product(c - 1)
+        last = len(Z_CHUNKS) - 1
+        z_gather(last, PACK - 2)
+        z_gather(last, PACK - 1)
+        z_bf[last] = weave(z[last], "z_bf%d" % last)
+        second_product(last)
+        for c in range(last):
+            for t in range(PACK):
+                h_copy(c, t)
+
+        out_rows = out_0.rearrange("(p t) j -> p t j", t=PACK)
+        out_words = out_1[0].rearrange("p c r -> p (c r)").bitcast(I32)
+        o_s = sb.tile([P, S], U8, name="o_s", align_bytes=64)
+        g4, g5, p04, p56, o = (chunk_tiles(name, OUT_CHUNKS) for name in ("g4_", "g5_", "p04_", "p56_", "o"))
+        units = [(c, t) for c in range(len(OUT_CHUNKS)) for t in (0, 2)]
+        o_bf = {}
+
+        def o_sum(c, t):
+            lo, hi = OUT_CHUNKS[c]
+            nc.vector.scalar_tensor_tensor(o[c][:, t : t + 2, :], p56[c][:, t : t + 2, :], 0.75, p04[c][:, t : t + 2, :], ALU.mult, ALU.add)
+            if t == PACK - 2:
+                nc.sync.dma_start(out_rows[:, :, lo:hi], o[c][:])
+
+        def planes(c):
+            lo, hi = OUT_CHUNKS[c]
+            o_w = sb.tile([P, hi - lo], I32, name="o_w%d" % c, align_bytes=64)
+            quantise(o_bf[c], o_w[:], o_s[:, lo:hi])
+            nc.sync.dma_start(out_words[:, lo:hi], o_w[:])
+
+        for u, (c, t0) in enumerate(units):
+            lo, hi = OUT_CHUNKS[c]
+            for t in (t0, t0 + 1):
+                if c == 0:
+                    h_copy(last, t)
+                nc.scalar.activation(g5[c][:, t, :], h[t][:].indirect(entries(n5_t, lo, hi)), COPY)
+                if (c, t) == (0, 0):
+                    nc.vector.tensor_copy(g4[c][:, t, :], h[t][:].indirect(entries(n4_t, lo, hi)))
+                else:
+                    nc.scalar.activation(g4[c][:, t, :], h[t][:].indirect(entries(n4_t, lo, hi)), COPY)
+                nc.vector.tensor_tensor(p56[c][:, t, :], h[t][:].indirect(entries(n6_t, lo, hi)), g5[c][:, t, :], ALU.mult)
+                if t == t0 and u > 0:
+                    o_sum(*units[u - 1])
+                nc.vector.scalar_tensor_tensor(p04[c][:, t, :], g4[c][:, t, :], 0.75, h[t][:, lo:hi], ALU.mult, ALU.mult)
+                if c > 0 and t == 0:
+                    o_bf[c - 1] = weave(o[c - 1], "o_bf%d" % (c - 1))
+                if c > 0 and t == 1:
+                    planes(c - 1)
+        last = len(OUT_CHUNKS) - 1
+        o_sum(last, PACK - 2)
+        o_bf[last] = weave(o[last], "o_bf%d" % last)
+        planes(last)
+        for q in range(4):
+            queue = nc.sync if q % 2 else nc.scalar
+            queue.dma_start(out_2[0, 4 * q : 4 * q + 4, :].bitcast(I32), o_s[32 * q : 32 * q + 4, :].bitcast(I32))

@@ -71,12 +71,15 @@ def tile_picked_mixhtrimdot_none_po_kernel(
                 stop=stop,
             )
 
-        def weave(src, name):
+        def woven_view(ap, run):
+            return ap.rearrange("p (c i) t -> p c t i", i=run)
+
+        def planar_view(ap, run):
+            return ap.rearrange("p t (c i) -> p c t i", i=run)
+
+        def weave(src, name, copy):
             woven = sb.tile([P, src.shape[2], PACK], BF16, name=name, align_bytes=64)
-            nc.vector.tensor_copy(
-                woven[:].rearrange("p (c i) t -> p c t i", i=4),
-                src[:].rearrange("p t (c i) -> p c t i", i=4),
-            )
+            copy(woven_view(woven[:], 4), planar_view(src[:], 4))
             return woven
 
         def quantise(woven, codes, scales):
@@ -85,32 +88,38 @@ def tile_picked_mixhtrimdot_none_po_kernel(
         xw = sb.tile([P, T], I32, name="xw")
         xs = sb.tile([P, T], U8, name="xs")
         w_raw = [sb.tile([P, 2 * H], U8, name="wraw%d" % i) for i in range(3)]
-        s_raw = [sb.tile([P, H], U8, name="sraw%d" % i) for i in range(3)]
+        s_raw = [sb.tile([P, H], U8, name="sraw%d" % i, tag="sraw%d" % i, align_bytes=64) for i in range(3)]
         gain = sb.tile([P, PACK], F32, name="gain")
 
-        offs_t = load_list(offs, "offs_t")
-        for q in range(3):
-            load_scale_quadrant(nc.scalar, xs, x_scales, q)
-        load_scale_quadrant(nc.sync, xs, x_scales, 3)
         nc.sync.dma_start(w_raw[0][:].bitcast(I32), w1_words[0].bitcast(I32))
-        nc.scalar.dma_start(xw[:], x_words[0].rearrange("p c r -> p (c r)").bitcast(I32))
-        for q in range(4):
-            load_scale_quadrant(nc.sync, s_raw[0], w1_scales, q)
+        offs_t = load_list(offs, "offs_t")
+        load_scale_quadrant(nc.scalar, xs, x_scales, 0)
+        load_scale_quadrant(nc.scalar, xs, x_scales, 1)
+        load_scale_quadrant(nc.scalar, xs, x_scales, 2)
+        load_scale_quadrant(nc.sync, xs, x_scales, 3)
         hz_t = load_list(hz, "hz_t")
+        nc.scalar.dma_start(xw[:], x_words[0].rearrange("p c r -> p (c r)").bitcast(I32))
+        load_scale_quadrant(nc.sync, s_raw[0], w1_scales, 0)
+        load_scale_quadrant(nc.sync, s_raw[0], w1_scales, 1)
+        load_scale_quadrant(nc.sync, s_raw[0], w1_scales, 2)
+        load_scale_quadrant(nc.sync, s_raw[0], w1_scales, 3)
         n2_t = load_list(n2, "n2_t")
         n3_t = load_list(n3, "n3_t")
-        nc.sync.dma_start(gain[:], gn.rearrange("(p t) o -> p (t o)", t=PACK))
+        nc.scalar.dma_start(gain[:], gn.rearrange("(p t) o -> p (t o)", t=PACK))
         n1_t = load_list(n1, "n1_t")
-        for i, (ww, ws) in ((2, (w3_words, w3_scales)), (1, (w2_words, w2_scales))):
-            nc.sync.dma_start(w_raw[i][:].bitcast(I32), ww[0].bitcast(I32))
-            for q in range(4):
-                load_scale_quadrant(nc.sync, s_raw[i], ws, q)
-        n5_t = load_list(n5, "n5_t")
-        n4_t = load_list(n4, "n4_t")
-        n6_t = load_list(n6, "n6_t")
+        nc.scalar.dma_start(w_raw[2][:].bitcast(I32), w3_words[0].bitcast(I32))
+        nc.scalar.dma_start(w_raw[1][:].bitcast(I32), w2_words[0].bitcast(I32))
+        load_scale_quadrant(nc.sync, s_raw[2], w3_scales, 0)
+        load_scale_quadrant(nc.sync, s_raw[2], w3_scales, 1)
+        load_scale_quadrant(nc.sync, s_raw[2], w3_scales, 2)
+        load_scale_quadrant(nc.sync, s_raw[2], w3_scales, 3)
+        load_scale_quadrant(nc.sync, s_raw[1], w2_scales, 0)
+        load_scale_quadrant(nc.sync, s_raw[1], w2_scales, 1)
+        load_scale_quadrant(nc.sync, s_raw[1], w2_scales, 2)
+        load_scale_quadrant(nc.sync, s_raw[1], w2_scales, 3)
 
         hz_scales = sb.tile([P, S], U8, name="hz_scales", align_bytes=64)
-        nc.gpsimd.memset(hz_scales[:], 0)
+        nc.vector.memset(hz_scales[:].bitcast(I32), 0)
 
         pick_s = sb.tile([P, S], U8, name="pick_s", align_bytes=64)
         nc.vector.tensor_copy(pick_s[:], xs[:].indirect(offs_t[:]))
@@ -128,7 +137,10 @@ def tile_picked_mixhtrimdot_none_po_kernel(
         for r in range(4):
             first = r if r < 2 else 16 + r
             nc.sync.dma_start(hz_scales[r:P:32, :].bitcast(I32), hz_raw[first:P:32, :].bitcast(I32))
-        hz_w = sb.tile([P, S], U32, name="hz_w", align_bytes=64)
+        n5_t = load_list(n5, "n5_t")
+        n4_t = load_list(n4, "n4_t")
+        n6_t = load_list(n6, "n6_t")
+        hz_w = sb.tile([P, S], U32, name="hz_w", tag="sraw0", align_bytes=64)
         nc.vector.tensor_copy(hz_w[:], xw[:].bitcast(U32).indirect(hz_t[:]))
         w3q = deal_words(w_raw[2], "w3q")
         w3s = deal_scales(s_raw[2], "w3s")
@@ -143,99 +155,128 @@ def tile_picked_mixhtrimdot_none_po_kernel(
             return [sb.tile([P, PACK, hi - lo], F32, name="%s%d" % (name, c)) for c, (lo, hi) in enumerate(chunks)]
 
         a, b, m, e, z = (chunk_tiles(name, Z_CHUNKS) for name in ("a", "b", "m", "e", "z"))
-        units = [(c, t) for c in range(len(Z_CHUNKS)) for t in (0, 2)]
-        z_bf = {}
+        units = [(c, t) for c in range(len(Z_CHUNKS)) for t in range(PACK)]
+        last = len(Z_CHUNKS) - 1
         h_ps = {}
+
+        def gather(on_vector, out, window, offsets):
+            if on_vector:
+                nc.vector.tensor_copy(out, window[:].indirect(offsets))
+            else:
+                nc.scalar.activation(out, window[:].indirect(offsets), COPY)
 
         def z_gather(c, t):
             lo, hi = Z_CHUNKS[c]
-            nc.vector.tensor_tensor(z[c][:, t, :], gy[t][:].indirect(entries(n1_t, lo, hi)), e[c][:, t, :], ALU.subtract)
+            if c not in (1, 2):
+                nc.vector.tensor_tensor(z[c][:, t, :], gy[t][:].indirect(entries(n1_t, lo, hi)), e[c][:, t, :], ALU.subtract)
 
-        def second_product(c):
+        def z_round(c):
+            if c in (1, 2):
+                woven = sb.tile([P, z[c].shape[2], PACK], BF16, name="z_bf%d" % c, align_bytes=64)
+                nc.vector.tensor_tensor(woven_view(woven[:], 2), planar_view(z[c][:], 2), planar_view(e[c][:], 2), ALU.subtract)
+                return woven
+            return weave(z[c], "z_bf%d" % c, nc.scalar.copy if c in () else nc.vector.tensor_copy)
+
+        def second_product(c, woven):
             lo, hi = Z_CHUNKS[c]
             w = hi - lo
             z_w = sb.tile([P, w], U32, name="z_w%d" % c, align_bytes=64)
             z_s = sb.tile([P, w], U8, name="z_s%d" % c, align_bytes=64)
-            quantise(z_bf[c], z_w[:], z_s[:])
-            for t in range(PACK):
-                h_ps[c, t] = psum.tile([P, S], F32, name="h_ps%d_%d" % (c, t), tag="bank%d" % (PACK * ((c + 1) % 2) + t))
-                mm(h_ps[c, t][:, 0:w], w3q, w3s, t, hz_w[:, lo:hi], hz_scales[:, lo:hi], True, False)
-            for t in range(PACK):
-                mm(h_ps[c, t][:, 0:w], w2q, w2s, t, z_w[:], z_s[:], False, True)
+            quantise(woven, z_w[:], z_s[:])
+            if c == last:
+                for t in range(PACK):
+                    h_ps[c, t] = psum.tile([P, S], F32, name="h_ps%d_%d" % (c, t), tag="bank%d" % t)[:, 0:w]
+                    mm(h_ps[c, t], w3q, w3s, t, hz_w[:, lo:hi], hz_scales[:, lo:hi], True, False)
+                for t in range(PACK):
+                    mm(h_ps[c, t], w2q, w2s, t, z_w[:], z_s[:], False, True)
+            else:
+                per_bank = S // w
+                for t in range(PACK):
+                    if t % per_bank == 0:
+                        bank = psum.tile([P, S], F32, name="h_ps%d_%d" % (c, t))
+                    h_ps[c, t] = bank[:, (t % per_bank) * w : (t % per_bank + 1) * w]
+                    mm(h_ps[c, t], w3q, w3s, t, hz_w[:, lo:hi], hz_scales[:, lo:hi], True, False)
+                    mm(h_ps[c, t], w2q, w2s, t, z_w[:], z_s[:], False, True)
 
-        def h_copy(c, t):
+        def h_copy(c, t, on_vector):
             lo, hi = Z_CHUNKS[c]
-            nc.scalar.activation(h[t][:, lo:hi], h_ps[c, t][:, 0 : hi - lo], COPY)
+            if on_vector:
+                nc.vector.tensor_copy(h[t][:, lo:hi], h_ps[c, t])
+            else:
+                nc.scalar.activation(h[t][:, lo:hi], h_ps[c, t], COPY)
 
-        for u, (c, t0) in enumerate(units):
+        for u, (c, t) in enumerate(units):
             lo, hi = Z_CHUNKS[c]
-            for t in (t0, t0 + 1):
-                if c == 0:
-                    nc.scalar.activation(y[t][:], y_ps[t][:], COPY)
-                nc.scalar.activation(a[c][:, t, :], y[t][:].indirect(entries(n2_t, lo, hi)), COPY)
-                nc.scalar.activation(b[c][:, t, :], y[t][:].indirect(entries(n3_t, lo, hi)), COPY)
-            for t in (t0, t0 + 1):
-                if c == 0:
-                    nc.scalar.activation(gy[t][:], y_ps[t][:], COPY, scale=gain[:, t : t + 1])
-            nc.vector.tensor_tensor(m[c][:, t0 : t0 + 2, :], a[c][:, t0 : t0 + 2, :], b[c][:, t0 : t0 + 2, :], ALU.max)
-            for d in (0, 1):
-                t = t0 + d
-                if u > 0:
-                    z_gather(units[u - 1][0], units[u - 1][1] + d)
-                nc.vector.scalar_tensor_tensor(e[c][:, t, :], m[c][:, t, :], gain[:, t : t + 1], gy[t][:, lo:hi], ALU.mult, ALU.subtract)
-            if c > 0 and t0 == 0:
-                z_bf[c - 1] = weave(z[c - 1], "z_bf%d" % (c - 1))
-                second_product(c - 1)
-        last = len(Z_CHUNKS) - 1
-        z_gather(last, PACK - 2)
+            if c == 0:
+                nc.scalar.activation(y[t][:], y_ps[t][:], COPY)
+            gather(False, a[c][:, t, :], y[t], entries(n2_t, lo, hi))
+            gather(u in (0, 1, 2), b[c][:, t, :], y[t], entries(n3_t, lo, hi))
+            if c == 0 and t in ():
+                nc.scalar.activation(gy[t][:], y_ps[t][:], COPY, scale=gain[:, t : t + 1])
+            elif c == 0:
+                nc.vector.tensor_scalar(gy[t][:], y[t][:], gain[:, t : t + 1], None, ALU.mult)
+            if c in (1, 2):
+                gather(False, z[c][:, t, :], gy[t], entries(n1_t, lo, hi))
+            nc.vector.tensor_tensor(m[c][:, t, :], a[c][:, t, :], b[c][:, t, :], ALU.max)
+            if u > 0:
+                z_gather(*units[u - 1])
+            if c > 0 and t == 1 and c - 1 not in ():
+                second_product(c - 1, woven)
+            nc.vector.scalar_tensor_tensor(e[c][:, t, :], m[c][:, t, :], gain[:, t : t + 1], gy[t][:, lo:hi], ALU.mult, ALU.subtract)
+            if c > 0 and t == 0 and c - 1 not in ():
+                woven = z_round(c - 1)
         z_gather(last, PACK - 1)
-        z_bf[last] = weave(z[last], "z_bf%d" % last)
-        second_product(last)
+        for c in ():
+            second_product(c, z_round(c))
+        second_product(last, z_round(last))
         for c in range(last):
             for t in range(PACK):
-                h_copy(c, t)
+                h_copy(c, t, False)
+        for t in range(PACK):
+            h_copy(last, t, t in ())
 
         out_rows = out_0.rearrange("(p t) j -> p t j", t=PACK)
         out_words = out_1[0].rearrange("p c r -> p (c r)").bitcast(I32)
         o_s = sb.tile([P, S], U8, name="o_s", align_bytes=64)
         g4, g5, p04, p56, o = (chunk_tiles(name, OUT_CHUNKS) for name in ("g4_", "g5_", "p04_", "p56_", "o"))
-        units = [(c, t) for c in range(len(OUT_CHUNKS)) for t in (0, 2)]
-        o_bf = {}
+        units = [(c, t) for c in range(len(OUT_CHUNKS)) for t in range(PACK)]
+        last = len(OUT_CHUNKS) - 1
 
         def o_sum(c, t):
             lo, hi = OUT_CHUNKS[c]
-            nc.vector.scalar_tensor_tensor(o[c][:, t : t + 2, :], p56[c][:, t : t + 2, :], 0.75, p04[c][:, t : t + 2, :], ALU.mult, ALU.add)
-            if t == PACK - 2:
+            if c not in (0, 1, 2):
+                nc.vector.scalar_tensor_tensor(o[c][:, t, :], p56[c][:, t, :], 0.75, p04[c][:, t, :], ALU.mult, ALU.add)
+            elif t % 2:
+                nc.vector.scalar_tensor_tensor(o[c][:, t - 1 : t + 1, :], p56[c][:, t - 1 : t + 1, :], 0.75, p04[c][:, t - 1 : t + 1, :], ALU.mult, ALU.add)
+            if t == PACK - 1:
                 nc.sync.dma_start(out_rows[:, :, lo:hi], o[c][:])
 
-        def planes(c):
+        def planes(c, woven):
             lo, hi = OUT_CHUNKS[c]
             o_w = sb.tile([P, hi - lo], I32, name="o_w%d" % c, align_bytes=64)
-            quantise(o_bf[c], o_w[:], o_s[:, lo:hi])
+            quantise(woven, o_w[:], o_s[:, lo:hi])
             nc.sync.dma_start(out_words[:, lo:hi], o_w[:])
 
-        for u, (c, t0) in enumerate(units):
+        for u, (c, t) in enumerate(units):
             lo, hi = OUT_CHUNKS[c]
-            for t in (t0, t0 + 1):
-                if c == 0:
-                    h_copy(last, t)
-                nc.scalar.activation(g5[c][:, t, :], h[t][:].indirect(entries(n5_t, lo, hi)), COPY)
-                if (c, t) == (0, 0):
-                    nc.vector.tensor_copy(g4[c][:, t, :], h[t][:].indirect(entries(n4_t, lo, hi)))
-                else:
-                    nc.scalar.activation(g4[c][:, t, :], h[t][:].indirect(entries(n4_t, lo, hi)), COPY)
-                nc.vector.tensor_tensor(p56[c][:, t, :], h[t][:].indirect(entries(n6_t, lo, hi)), g5[c][:, t, :], ALU.mult)
-                if t == t0 and u > 0:
-                    o_sum(*units[u - 1])
-                nc.vector.scalar_tensor_tensor(p04[c][:, t, :], g4[c][:, t, :], 0.75, h[t][:, lo:hi], ALU.mult, ALU.mult)
-                if c > 0 and t == 0:
-                    o_bf[c - 1] = weave(o[c - 1], "o_bf%d" % (c - 1))
-                if c > 0 and t == 1:
-                    planes(c - 1)
-        last = len(OUT_CHUNKS) - 1
-        o_sum(last, PACK - 2)
-        o_bf[last] = weave(o[last], "o_bf%d" % last)
-        planes(last)
+            pieces = [(x, min(x + 256, hi)) for x in range(lo, hi, 256)]
+            for x0, x1 in pieces:
+                gather(False, g5[c][:, t, x0 - lo : x1 - lo], h[t], entries(n5_t, x0, x1))
+            for x0, x1 in pieces:
+                gather((u, x0) in ((0, 0), (1, 0)), g4[c][:, t, x0 - lo : x1 - lo], h[t], entries(n4_t, x0, x1))
+            for x0, x1 in pieces:
+                nc.vector.tensor_tensor(p56[c][:, t, x0 - lo : x1 - lo], h[t][:].indirect(entries(n6_t, x0, x1)), g5[c][:, t, x0 - lo : x1 - lo], ALU.mult)
+            if c > 0 and t == 1 and c - 1 not in (0,):
+                woven = weave(o[c - 1], "o_bf%d" % (c - 1), nc.vector.tensor_copy)
+            nc.vector.scalar_tensor_tensor(p04[c][:, t, :], g4[c][:, t, :], 0.75, h[t][:, lo:hi], ALU.mult, ALU.mult)
+            if c > 0 and t == 1 and c - 1 not in (0,):
+                planes(c - 1, woven)
+            if u > 0:
+                o_sum(*units[u - 1])
+        for c in (0,):
+            planes(c, weave(o[c], "o_bf%d" % c, nc.scalar.copy))
+        o_sum(last, PACK - 1)
+        planes(last, weave(o[last], "o_bf%d" % last, nc.vector.tensor_copy))
         for q in range(4):
             queue = nc.sync if q % 2 else nc.scalar
             queue.dma_start(out_2[0, 4 * q : 4 * q + 4, :].bitcast(I32), o_s[32 * q : 32 * q + 4, :].bitcast(I32))

@@ -18,8 +18,22 @@ COPY = mybir.ActivationFunctionType.Copy
 
 P = 128
 PACK = 4
-Z_CHUNKS = ((0, 256), (256, 384), (384, 512))
-OUT_CHUNKS = ((0, 256), (256, 384), (384, 512))
+QUADS = 4
+HALF = S // 2
+LAST = PACK - 1
+OUT_FACTOR = 0.75
+
+WIDE = 2 * S
+STAGES = ((0, HALF), (HALF, HALF + P), (HALF + P, S))
+Z_UNITS = (
+    [(0, 0, S)]
+    + [(t, 0, HALF) for t in range(1, PACK)]
+    + [(t, HALF, S) for t in range(1, LAST)]
+    + [(LAST, lo, hi) for lo, hi in STAGES[1:]]
+)
+OUT_UNITS = [(t, 0, S) for t in range(LAST)] + [(LAST, lo, hi) for lo, hi in STAGES]
+VECTOR_N3 = 3
+FUSED_N4 = (S, HALF, 0, 0)
 
 
 def tile_picked_mixhtrimdot_none_po_kernel(
@@ -33,38 +47,34 @@ def tile_picked_mixhtrimdot_none_po_kernel(
         psum = ctx.enter_context(tc.psum_pool(name="psum", bufs=1))
 
         def load_list(src, name):
-            tl = lists.tile([P, S // 16], U16, name=name)
-            nc.sync.dma_start(tl[:], src)
-            return tl
+            offsets = lists.tile([P, S // 16], U16, name=name)
+            nc.sync.dma_start(offsets[:], src)
+            return offsets
 
-        def load_scale_quadrant(queue, tl, src, q):
-            rows = src[0, 4 * q : 4 * q + 4, :].bitcast(I32)
-            queue.dma_start(tl[32 * q : 32 * q + 32, :].bitcast(I32), rows.partition_broadcast(8))
+        def load_words(queue, raw, src):
+            queue.dma_start(raw[:].bitcast(I32), src[0].bitcast(I32))
 
-        def entries(lst, lo, hi):
-            return lst[:, lo // 16 : hi // 16]
+        def load_scales(queue, raw, src, quads):
+            for q in quads:
+                rows = src[0, 4 * q : 4 * q + 4, :].bitcast(I32)
+                queue.dma_start(raw[32 * q : 32 * q + 32, :].bitcast(I32), rows.partition_broadcast(8))
 
-        def deal_words(raw, name):
-            dealt = sb.tile([P, 2 * H], U8, name=name, align_bytes=64)
+        def entries(offsets, lo, hi):
+            return offsets[:, lo // 16 : hi // 16]
+
+        def deal(raw, name, dtype):
+            dealt = sb.tile(list(raw.shape), U8, name=name, align_bytes=64)
             nc.vector.tensor_copy(
-                dealt[:].bitcast(U16).rearrange("p (t m) -> p t m", t=PACK),
-                raw[:].bitcast(U16).rearrange("p (m t) -> p t m", t=PACK),
+                dealt[:].bitcast(dtype).rearrange("p (t m) -> p t m", t=PACK),
+                raw[:].bitcast(dtype).rearrange("p (m t) -> p t m", t=PACK),
             )
             return dealt
 
-        def deal_scales(raw, name):
-            dealt = sb.tile([P, H], U8, name=name, align_bytes=64)
-            nc.vector.tensor_copy(
-                dealt[:].rearrange("p (t m) -> p t m", t=PACK),
-                raw[:].rearrange("p (m t) -> p t m", t=PACK),
-            )
-            return dealt
-
-        def mm(acc, wq, ws, t, codes, scales, start, stop):
+        def multiply(acc, w_codes, w_scales, t, codes, scales, start, stop):
             nc.tensor.matmul_mx(
                 out=acc,
-                lhsT=wq[:, 2 * P * t : 2 * P * (t + 1)].bitcast(FP4X4),
-                lhsT_scale=ws[:, P * t : P * (t + 1)],
+                lhsT=w_codes[:, 2 * P * t : 2 * P * (t + 1)].bitcast(FP4X4),
+                lhsT_scale=w_scales[:, P * t : P * (t + 1)],
                 rhs=codes.bitcast(FP8X4),
                 rhs_scale=scales,
                 start=start,
@@ -79,204 +89,204 @@ def tile_picked_mixhtrimdot_none_po_kernel(
 
         def weave(src, name, copy):
             woven = sb.tile([P, src.shape[2], PACK], BF16, name=name, align_bytes=64)
-            copy(woven_view(woven[:], 4), planar_view(src[:], 4))
+            copy(woven_view(woven[:], 4), planar_view(src, 4))
             return woven
 
         def quantise(woven, codes, scales):
             nc.vector.quantize_mx(out=codes.bitcast(FP8X4), scales=scales, in_=woven[:].rearrange("p j t -> p (j t)"))
 
-        xw = sb.tile([P, T], I32, name="xw")
-        xs = sb.tile([P, T], U8, name="xs")
-        w_raw = [sb.tile([P, 2 * H], U8, name="wraw%d" % i) for i in range(3)]
-        s_raw = [sb.tile([P, H], U8, name="sraw%d" % i, tag="sraw%d" % i, align_bytes=64) for i in range(3)]
+        def fetch_on_scalar(out, window, offsets):
+            nc.scalar.activation(out, window[:].indirect(offsets), COPY)
+
+        def planar(name, width=S):
+            return sb.tile([P, PACK, width], F32, name=name)
+
+        x_codes = sb.tile([P, T], I32, name="x_codes")
+        x_rows = sb.tile([P, T], U8, name="x_rows")
+        w1_raw, w2_raw, w3_raw = (sb.tile([P, 2 * H], U8, name="w%d_raw" % i) for i in (1, 2, 3))
+        s1_raw, s2_raw, s3_raw = (
+            sb.tile([P, H], U8, name="s%d_raw" % i, tag="s%d_raw" % i, align_bytes=64) for i in (1, 2, 3)
+        )
         gain = sb.tile([P, PACK], F32, name="gain")
 
-        nc.sync.dma_start(w_raw[0][:].bitcast(I32), w1_words[0].bitcast(I32))
+        load_words(nc.sync, w1_raw, w1_words)
         offs_t = load_list(offs, "offs_t")
-        load_scale_quadrant(nc.scalar, xs, x_scales, 0)
-        load_scale_quadrant(nc.scalar, xs, x_scales, 1)
-        load_scale_quadrant(nc.scalar, xs, x_scales, 2)
-        load_scale_quadrant(nc.sync, xs, x_scales, 3)
+        load_scales(nc.scalar, x_rows, x_scales, range(QUADS - 1))
+        load_scales(nc.sync, x_rows, x_scales, [QUADS - 1])
         hz_t = load_list(hz, "hz_t")
-        nc.scalar.dma_start(xw[:], x_words[0].rearrange("p c r -> p (c r)").bitcast(I32))
-        load_scale_quadrant(nc.sync, s_raw[0], w1_scales, 0)
-        load_scale_quadrant(nc.sync, s_raw[0], w1_scales, 1)
-        load_scale_quadrant(nc.sync, s_raw[0], w1_scales, 2)
-        load_scale_quadrant(nc.sync, s_raw[0], w1_scales, 3)
+        nc.scalar.dma_start(x_codes[:], x_words[0].rearrange("p c r -> p (c r)").bitcast(I32))
+        load_scales(nc.sync, s1_raw, w1_scales, range(QUADS))
         n2_t = load_list(n2, "n2_t")
         n3_t = load_list(n3, "n3_t")
         nc.scalar.dma_start(gain[:], gn.rearrange("(p t) o -> p (t o)", t=PACK))
         n1_t = load_list(n1, "n1_t")
-        nc.scalar.dma_start(w_raw[2][:].bitcast(I32), w3_words[0].bitcast(I32))
-        nc.scalar.dma_start(w_raw[1][:].bitcast(I32), w2_words[0].bitcast(I32))
-        load_scale_quadrant(nc.sync, s_raw[2], w3_scales, 0)
-        load_scale_quadrant(nc.sync, s_raw[2], w3_scales, 1)
-        load_scale_quadrant(nc.sync, s_raw[2], w3_scales, 2)
-        load_scale_quadrant(nc.sync, s_raw[2], w3_scales, 3)
-        load_scale_quadrant(nc.sync, s_raw[1], w2_scales, 0)
-        load_scale_quadrant(nc.sync, s_raw[1], w2_scales, 1)
-        load_scale_quadrant(nc.sync, s_raw[1], w2_scales, 2)
-        load_scale_quadrant(nc.sync, s_raw[1], w2_scales, 3)
+        load_words(nc.scalar, w3_raw, w3_words)
+        load_words(nc.scalar, w2_raw, w2_words)
+        load_scales(nc.sync, s3_raw, w3_scales, range(QUADS))
+        load_scales(nc.sync, s2_raw, w2_scales, range(QUADS))
 
         hz_scales = sb.tile([P, S], U8, name="hz_scales", align_bytes=64)
         nc.vector.memset(hz_scales[:].bitcast(I32), 0)
 
-        pick_s = sb.tile([P, S], U8, name="pick_s", align_bytes=64)
-        nc.vector.tensor_copy(pick_s[:], xs[:].indirect(offs_t[:]))
-        w1q = deal_words(w_raw[0], "w1q")
-        w1s = deal_scales(s_raw[0], "w1s")
-        pick_w = sb.tile([P, S], U32, name="pick_w", align_bytes=64)
-        nc.vector.tensor_copy(pick_w[:], xw[:].bitcast(U32).indirect(offs_t[:]))
+        pick_scales = sb.tile([P, S], U8, name="pick_scales", align_bytes=64)
+        nc.vector.tensor_copy(pick_scales[:], x_rows[:].indirect(offs_t[:]))
+        w1_codes = deal(w1_raw, "w1_codes", U16)
+        w1_bytes = deal(s1_raw, "w1_bytes", U8)
+        pick_codes = sb.tile([P, S], U32, name="pick_codes", align_bytes=64)
+        nc.vector.tensor_copy(pick_codes[:], x_codes[:].bitcast(U32).indirect(offs_t[:]))
 
         y_ps = [psum.tile([P, S], F32, name="y_ps%d" % t, tag="bank%d" % t) for t in range(PACK)]
         for t in range(PACK):
-            mm(y_ps[t][:], w1q, w1s, t, pick_w[:], pick_s[:], True, True)
+            multiply(y_ps[t][:], w1_codes, w1_bytes, t, pick_codes[:], pick_scales[:], True, True)
 
-        hz_raw = sb.tile([P, S], U8, name="hz_raw")
-        nc.vector.tensor_copy(hz_raw[:], xs[:].indirect(hz_t[:]))
+        hz_rows = sb.tile([P, S], U8, name="hz_rows")
+        nc.vector.tensor_copy(hz_rows[:], x_rows[:].indirect(hz_t[:]))
         for r in range(4):
             first = r if r < 2 else 16 + r
-            nc.sync.dma_start(hz_scales[r:P:32, :].bitcast(I32), hz_raw[first:P:32, :].bitcast(I32))
+            nc.sync.dma_start(hz_scales[r:P:32, :].bitcast(I32), hz_rows[first:P:32, :].bitcast(I32))
         n5_t = load_list(n5, "n5_t")
         n4_t = load_list(n4, "n4_t")
         n6_t = load_list(n6, "n6_t")
-        hz_w = sb.tile([P, S], U32, name="hz_w", tag="sraw0", align_bytes=64)
-        nc.vector.tensor_copy(hz_w[:], xw[:].bitcast(U32).indirect(hz_t[:]))
-        w3q = deal_words(w_raw[2], "w3q")
-        w3s = deal_scales(s_raw[2], "w3s")
-        w2q = deal_words(w_raw[1], "w2q")
-        w2s = deal_scales(s_raw[1], "w2s")
+        hz_codes = sb.tile([P, S], U32, name="hz_codes", tag="s1_raw", align_bytes=64)
+        nc.vector.tensor_copy(hz_codes[:], x_codes[:].bitcast(U32).indirect(hz_t[:]))
+        w3_codes = deal(w3_raw, "w3_codes", U16)
+        w3_bytes = deal(s3_raw, "w3_bytes", U8)
+        w2_codes = deal(w2_raw, "w2_codes", U16)
+        w2_bytes = deal(s2_raw, "w2_bytes", U8)
 
-        y = [sb.tile([P, S], F32, name="y%d" % t) for t in range(PACK)]
+        y = [sb.tile([P, WIDE if t == 0 else S], F32, name="y%d" % t) for t in range(PACK)]
+        nc.vector.memset(y[0][:, S:WIDE], 0.0)
         gy = [sb.tile([P, S], F32, name="gy%d" % t) for t in range(PACK)]
-        h = [sb.tile([P, S], F32, name="h%d" % t) for t in range(PACK)]
-
-        def chunk_tiles(name, chunks):
-            return [sb.tile([P, PACK, hi - lo], F32, name="%s%d" % (name, c)) for c, (lo, hi) in enumerate(chunks)]
-
-        a, b, m, e, z = (chunk_tiles(name, Z_CHUNKS) for name in ("a", "b", "m", "e", "z"))
-        units = [(c, t) for c in range(len(Z_CHUNKS)) for t in range(PACK)]
-        last = len(Z_CHUNKS) - 1
+        h = [sb.tile([P, WIDE if t < LAST else S], F32, name="h%d" % t) for t in range(PACK)]
+        larger = [h[t][:, S:WIDE] for t in range(LAST)] + [sb.tile([P, S], F32, name="larger_last")[:]]
+        y_n2, y_n3, rest = planar("y_n2"), planar("y_n3"), planar("rest")
+        z_first = planar("z_first", HALF)
+        gy_n1 = planar("gy_n1", HALF)
         h_ps = {}
 
-        def gather(on_vector, out, window, offsets):
-            if on_vector:
-                nc.vector.tensor_copy(out, window[:].indirect(offsets))
-            else:
-                nc.scalar.activation(out, window[:].indirect(offsets), COPY)
+        def round_z(stage):
+            lo, hi = STAGES[stage]
+            if stage == 0:
+                return weave(z_first[:], "z_bf0", nc.vector.tensor_copy)
+            woven = sb.tile([P, hi - lo, PACK], BF16, name="z_bf%d" % stage, align_bytes=64)
+            looked_up = gy_n1[:, :, lo - HALF : hi - HALF]
+            nc.vector.tensor_tensor(
+                woven_view(woven[:], 2), planar_view(looked_up, 2), planar_view(rest[:, :, lo:hi], 2), ALU.subtract
+            )
+            return woven
 
-        def z_gather(c, t):
-            lo, hi = Z_CHUNKS[c]
-            if c not in (1, 2):
-                nc.vector.tensor_tensor(z[c][:, t, :], gy[t][:].indirect(entries(n1_t, lo, hi)), e[c][:, t, :], ALU.subtract)
-
-        def z_round(c):
-            if c in (1, 2):
-                woven = sb.tile([P, z[c].shape[2], PACK], BF16, name="z_bf%d" % c, align_bytes=64)
-                nc.vector.tensor_tensor(woven_view(woven[:], 2), planar_view(z[c][:], 2), planar_view(e[c][:], 2), ALU.subtract)
-                return woven
-            return weave(z[c], "z_bf%d" % c, nc.scalar.copy if c in () else nc.vector.tensor_copy)
-
-        def second_product(c, woven):
-            lo, hi = Z_CHUNKS[c]
-            w = hi - lo
-            z_w = sb.tile([P, w], U32, name="z_w%d" % c, align_bytes=64)
-            z_s = sb.tile([P, w], U8, name="z_s%d" % c, align_bytes=64)
-            quantise(woven, z_w[:], z_s[:])
-            if c == last:
+        def second_product(stage, woven):
+            lo, hi = STAGES[stage]
+            z_codes = sb.tile([P, hi - lo], U32, name="z_codes%d" % stage, align_bytes=64)
+            z_scales = sb.tile([P, hi - lo], U8, name="z_scales%d" % stage, align_bytes=64)
+            quantise(woven, z_codes[:], z_scales[:])
+            half, start = divmod(lo, HALF)
+            if start == 0:
+                cols = slice(lo, lo + HALF)
                 for t in range(PACK):
-                    h_ps[c, t] = psum.tile([P, S], F32, name="h_ps%d_%d" % (c, t), tag="bank%d" % t)[:, 0:w]
-                    mm(h_ps[c, t], w3q, w3s, t, hz_w[:, lo:hi], hz_scales[:, lo:hi], True, False)
-                for t in range(PACK):
-                    mm(h_ps[c, t], w2q, w2s, t, z_w[:], z_s[:], False, True)
-            else:
-                per_bank = S // w
-                for t in range(PACK):
-                    if t % per_bank == 0:
-                        bank = psum.tile([P, S], F32, name="h_ps%d_%d" % (c, t))
-                    h_ps[c, t] = bank[:, (t % per_bank) * w : (t % per_bank + 1) * w]
-                    mm(h_ps[c, t], w3q, w3s, t, hz_w[:, lo:hi], hz_scales[:, lo:hi], True, False)
-                    mm(h_ps[c, t], w2q, w2s, t, z_w[:], z_s[:], False, True)
-
-        def h_copy(c, t, on_vector):
-            lo, hi = Z_CHUNKS[c]
-            if on_vector:
-                nc.vector.tensor_copy(h[t][:, lo:hi], h_ps[c, t])
-            else:
-                nc.scalar.activation(h[t][:, lo:hi], h_ps[c, t], COPY)
-
-        for u, (c, t) in enumerate(units):
-            lo, hi = Z_CHUNKS[c]
-            if c == 0:
-                nc.scalar.activation(y[t][:], y_ps[t][:], COPY)
-            gather(False, a[c][:, t, :], y[t], entries(n2_t, lo, hi))
-            gather(u in (0, 1, 2), b[c][:, t, :], y[t], entries(n3_t, lo, hi))
-            if c == 0 and t in ():
-                nc.scalar.activation(gy[t][:], y_ps[t][:], COPY, scale=gain[:, t : t + 1])
-            elif c == 0:
-                nc.vector.tensor_scalar(gy[t][:], y[t][:], gain[:, t : t + 1], None, ALU.mult)
-            if c in (1, 2):
-                gather(False, z[c][:, t, :], gy[t], entries(n1_t, lo, hi))
-            nc.vector.tensor_tensor(m[c][:, t, :], a[c][:, t, :], b[c][:, t, :], ALU.max)
-            if u > 0:
-                z_gather(*units[u - 1])
-            if c > 0 and t == 1 and c - 1 not in ():
-                second_product(c - 1, woven)
-            nc.vector.scalar_tensor_tensor(e[c][:, t, :], m[c][:, t, :], gain[:, t : t + 1], gy[t][:, lo:hi], ALU.mult, ALU.subtract)
-            if c > 0 and t == 0 and c - 1 not in ():
-                woven = z_round(c - 1)
-        z_gather(last, PACK - 1)
-        for c in ():
-            second_product(c, z_round(c))
-        second_product(last, z_round(last))
-        for c in range(last):
+                    bank = "bank%d" % (t + PACK * (1 - half))
+                    h_ps[half, t] = psum.tile([P, S], F32, name="h_ps%d_%d" % (half, t), tag=bank)[:, 0:HALF]
+                    multiply(h_ps[half, t], w3_codes, w3_bytes, t, hz_codes[:, cols], hz_scales[:, cols], True, False)
             for t in range(PACK):
-                h_copy(c, t, False)
+                acc = h_ps[half, t][:, start : start + hi - lo]
+                multiply(acc, w2_codes, w2_bytes, t, z_codes[:], z_scales[:], False, hi % HALF == 0)
+
+        rounded = None
+        for u, (t, lo, hi) in enumerate(Z_UNITS):
+            if lo == 0:
+                nc.scalar.activation(y[t][:, 0:S], y_ps[t][:], COPY)
+            fetch_on_scalar(y_n2[:, t, lo:hi], y[t], entries(n2_t, lo, hi))
+            if u < VECTOR_N3:
+                nc.vector.tensor_copy(y_n3[:, t, lo:hi], y[t][:].indirect(entries(n3_t, lo, hi)))
+            else:
+                fetch_on_scalar(y_n3[:, t, lo:hi], y[t], entries(n3_t, lo, hi))
+            if lo == 0:
+                nc.vector.tensor_scalar(gy[t][:], y[t][:, 0:S], gain[:, t : t + 1], None, ALU.mult)
+            if hi > HALF:
+                first = max(lo, HALF)
+                fetch_on_scalar(gy_n1[:, t, first - HALF : hi - HALF], gy[t], entries(n1_t, first, hi))
+            nc.vector.tensor_tensor(larger[t][:, lo:hi], y_n2[:, t, lo:hi], y_n3[:, t, lo:hi], ALU.max)
+            if 0 < u <= PACK:
+                before = u - 1
+                nc.vector.tensor_tensor(
+                    z_first[:, before, :],
+                    gy[before][:].indirect(entries(n1_t, 0, HALF)),
+                    rest[:, before, 0:HALF],
+                    ALU.subtract,
+                )
+            if rounded:
+                second_product(*rounded)
+                rounded = None
+            nc.vector.scalar_tensor_tensor(
+                rest[:, t, lo:hi], larger[t][:, lo:hi], gain[:, t : t + 1], gy[t][:, lo:hi], ALU.mult, ALU.subtract
+            )
+            if u == PACK:
+                rounded = (0, round_z(0))
+            if lo > 0 and t == LAST:
+                stage = STAGES.index((lo, hi))
+                rounded = (stage, round_z(stage))
+        second_product(*rounded)
+
+        scaled_h = planar("scaled_h")
+
+        def scale_h(half):
+            for t in range(PACK):
+                if FUSED_N4[t] > half * HALF:
+                    cols = slice(half * HALF, (half + 1) * HALF)
+                    nc.scalar.activation(scaled_h[:, t, cols], h_ps[half, t], COPY, scale=OUT_FACTOR)
+
         for t in range(PACK):
-            h_copy(last, t, t in ())
+            nc.scalar.activation(h[t][:, 0:HALF], h_ps[0, t], COPY)
+        scale_h(0)
+        for t in range(PACK):
+            if t % 2 == 0:
+                nc.vector.tensor_copy(h[t][:, HALF:S], h_ps[1, t])
+            else:
+                nc.scalar.activation(h[t][:, HALF:S], h_ps[1, t], COPY)
+        scale_h(1)
 
         out_rows = out_0.rearrange("(p t) j -> p t j", t=PACK)
         out_words = out_1[0].rearrange("p c r -> p (c r)").bitcast(I32)
-        o_s = sb.tile([P, S], U8, name="o_s", align_bytes=64)
-        g4, g5, p04, p56, o = (chunk_tiles(name, OUT_CHUNKS) for name in ("g4_", "g5_", "p04_", "p56_", "o"))
-        units = [(c, t) for c in range(len(OUT_CHUNKS)) for t in range(PACK)]
-        last = len(OUT_CHUNKS) - 1
+        out_codes = sb.tile([P, S], I32, name="out_codes", align_bytes=64)
+        out_scales = sb.tile([P, S], U8, name="out_scales", align_bytes=64)
+        h_n4, h_n5, h_n6, own, pair, result = (planar(name) for name in ("h_n4", "h_n5", "h_n6", "own", "pair", "result"))
 
-        def o_sum(c, t):
-            lo, hi = OUT_CHUNKS[c]
-            if c not in (0, 1, 2):
-                nc.vector.scalar_tensor_tensor(o[c][:, t, :], p56[c][:, t, :], 0.75, p04[c][:, t, :], ALU.mult, ALU.add)
-            elif t % 2:
-                nc.vector.scalar_tensor_tensor(o[c][:, t - 1 : t + 1, :], p56[c][:, t - 1 : t + 1, :], 0.75, p04[c][:, t - 1 : t + 1, :], ALU.mult, ALU.add)
-            if t == PACK - 1:
-                nc.sync.dma_start(out_rows[:, :, lo:hi], o[c][:])
+        def finish(t, lo, hi):
+            nc.vector.scalar_tensor_tensor(
+                result[:, t, lo:hi], pair[:, t, lo:hi], OUT_FACTOR, own[:, t, lo:hi], ALU.mult, ALU.add
+            )
+            if hi % HALF == 0:
+                stored = slice(lo // HALF * HALF, hi)
+                nc.sync.dma_start(out_rows[:, t, stored], result[:, t, stored])
+            if t == LAST:
+                copy = nc.scalar.copy if lo == 0 else nc.vector.tensor_copy
+                woven = weave(result[:, :, lo:hi], "out_bf%d" % lo, copy)
+                quantise(woven, out_codes[:, lo:hi], out_scales[:, lo:hi])
+                nc.sync.dma_start(out_words[:, lo:hi], out_codes[:, lo:hi])
 
-        def planes(c, woven):
-            lo, hi = OUT_CHUNKS[c]
-            o_w = sb.tile([P, hi - lo], I32, name="o_w%d" % c, align_bytes=64)
-            quantise(woven, o_w[:], o_s[:, lo:hi])
-            nc.sync.dma_start(out_words[:, lo:hi], o_w[:])
-
-        for u, (c, t) in enumerate(units):
-            lo, hi = OUT_CHUNKS[c]
-            pieces = [(x, min(x + 256, hi)) for x in range(lo, hi, 256)]
-            for x0, x1 in pieces:
-                gather(False, g5[c][:, t, x0 - lo : x1 - lo], h[t], entries(n5_t, x0, x1))
-            for x0, x1 in pieces:
-                gather((u, x0) in ((0, 0), (1, 0)), g4[c][:, t, x0 - lo : x1 - lo], h[t], entries(n4_t, x0, x1))
-            for x0, x1 in pieces:
-                nc.vector.tensor_tensor(p56[c][:, t, x0 - lo : x1 - lo], h[t][:].indirect(entries(n6_t, x0, x1)), g5[c][:, t, x0 - lo : x1 - lo], ALU.mult)
-            if c > 0 and t == 1 and c - 1 not in (0,):
-                woven = weave(o[c - 1], "o_bf%d" % (c - 1), nc.vector.tensor_copy)
-            nc.vector.scalar_tensor_tensor(p04[c][:, t, :], g4[c][:, t, :], 0.75, h[t][:, lo:hi], ALU.mult, ALU.mult)
-            if c > 0 and t == 1 and c - 1 not in (0,):
-                planes(c - 1, woven)
+        for u, (t, lo, hi) in enumerate(OUT_UNITS):
+            split = max(lo, FUSED_N4[t])
+            fetch_on_scalar(h_n5[:, t, lo:hi], h[t], entries(n5_t, lo, hi))
+            if lo < split:
+                nc.vector.tensor_tensor(
+                    own[:, t, lo:split], h[t][:].indirect(entries(n4_t, lo, split)), scaled_h[:, t, lo:split], ALU.mult
+                )
+            if split < hi:
+                fetch_on_scalar(h_n4[:, t, split:hi], h[t], entries(n4_t, split, hi))
+            if lo == 0:
+                nc.vector.tensor_tensor(
+                    pair[:, t, lo:hi], h[t][:].indirect(entries(n6_t, lo, hi)), h_n5[:, t, lo:hi], ALU.mult
+                )
+            else:
+                fetch_on_scalar(h_n6[:, t, lo:hi], h[t], entries(n6_t, lo, hi))
+                nc.vector.tensor_tensor(pair[:, t, lo:hi], h_n6[:, t, lo:hi], h_n5[:, t, lo:hi], ALU.mult)
+            if split < hi:
+                nc.vector.scalar_tensor_tensor(
+                    own[:, t, split:hi], h_n4[:, t, split:hi], OUT_FACTOR, h[t][:, split:hi], ALU.mult, ALU.mult
+                )
             if u > 0:
-                o_sum(*units[u - 1])
-        for c in (0,):
-            planes(c, weave(o[c], "o_bf%d" % c, nc.scalar.copy))
-        o_sum(last, PACK - 1)
-        planes(last, weave(o[last], "o_bf%d" % last, nc.vector.tensor_copy))
-        for q in range(4):
+                finish(*OUT_UNITS[u - 1])
+        finish(*OUT_UNITS[-1])
+        for q in range(QUADS):
             queue = nc.sync if q % 2 else nc.scalar
-            queue.dma_start(out_2[0, 4 * q : 4 * q + 4, :].bitcast(I32), o_s[32 * q : 32 * q + 4, :].bitcast(I32))
+            queue.dma_start(out_2[0, 4 * q : 4 * q + 4, :].bitcast(I32), out_scales[32 * q : 32 * q + 4, :].bitcast(I32))

@@ -51,13 +51,17 @@ def tile_picked_mixhtrimdot_none_po_kernel(
             nc.sync.dma_start(offsets[:], src)
             return offsets
 
-        def load_words(queue, raw, src):
-            queue.dma_start(raw[:].bitcast(I32), src[0].bitcast(I32))
+        def load_words(raw, src):
+            nc.sync.dma_start(raw[:].bitcast(I32), src[0].bitcast(I32))
 
-        def load_scales(queue, raw, src, quads):
-            for q in quads:
+        def load_scales(raw, src):
+            for q in range(QUADS):
                 rows = src[0, 4 * q : 4 * q + 4, :].bitcast(I32)
-                queue.dma_start(raw[32 * q : 32 * q + 32, :].bitcast(I32), rows.partition_broadcast(8))
+                nc.sync.dma_start(raw[32 * q : 32 * q + 4, :].bitcast(I32), rows)
+
+        def place_scales(queue, scales, rows):
+            for r in range(4):
+                queue.dma_start(scales[r:P:32, :].bitcast(I32), rows[8 * r : P : 32, :].bitcast(I32))
 
         def entries(offsets, lo, hi):
             return offsets[:, lo // 16 : hi // 16]
@@ -103,33 +107,37 @@ def tile_picked_mixhtrimdot_none_po_kernel(
 
         x_codes = sb.tile([P, T], I32, name="x_codes")
         x_rows = sb.tile([P, T], U8, name="x_rows")
-        w1_raw, w2_raw, w3_raw = (sb.tile([P, 2 * H], U8, name="w%d_raw" % i) for i in (1, 2, 3))
+        w1_raw, w2_raw, w3_raw = (
+            sb.tile([P, 2 * H], U8, name="w%d_raw" % i, tag="w%d_raw" % i, align_bytes=64) for i in (1, 2, 3)
+        )
         s1_raw, s2_raw, s3_raw = (
             sb.tile([P, H], U8, name="s%d_raw" % i, tag="s%d_raw" % i, align_bytes=64) for i in (1, 2, 3)
         )
+        pick_scales = sb.tile([P, S], U8, name="pick_scales", align_bytes=64)
+        hz_scales = sb.tile([P, S], U8, name="hz_scales", align_bytes=64)
         gain = sb.tile([P, PACK], F32, name="gain")
+        for scales in (s1_raw, pick_scales, s3_raw, s2_raw, hz_scales):
+            nc.vector.memset(scales[:].bitcast(I32), 0)
 
-        load_words(nc.sync, w1_raw, w1_words)
         offs_t = load_list(offs, "offs_t")
-        load_scales(nc.scalar, x_rows, x_scales, range(QUADS - 1))
-        load_scales(nc.sync, x_rows, x_scales, [QUADS - 1])
+        x_scale_rows = x_scales[0].bitcast(I32).unsqueeze(1).broadcast_to([P // 8, 8, T // 4])
+        nc.scalar.dma_start(x_rows[:].bitcast(I32), x_scale_rows)
         hz_t = load_list(hz, "hz_t")
+        load_scales(s1_raw, w1_scales)
         nc.scalar.dma_start(x_codes[:], x_words[0].rearrange("p c r -> p (c r)").bitcast(I32))
-        load_scales(nc.sync, s1_raw, w1_scales, range(QUADS))
+        load_words(w1_raw, w1_words)
         n2_t = load_list(n2, "n2_t")
         n3_t = load_list(n3, "n3_t")
-        nc.scalar.dma_start(gain[:], gn.rearrange("(p t) o -> p (t o)", t=PACK))
+        nc.sync.dma_start(gain[:], gn.rearrange("(p t) o -> p (t o)", t=PACK))
         n1_t = load_list(n1, "n1_t")
-        load_words(nc.scalar, w3_raw, w3_words)
-        load_words(nc.scalar, w2_raw, w2_words)
-        load_scales(nc.sync, s3_raw, w3_scales, range(QUADS))
-        load_scales(nc.sync, s2_raw, w2_scales, range(QUADS))
+        load_words(w3_raw, w3_words)
+        load_words(w2_raw, w2_words)
+        load_scales(s3_raw, w3_scales)
+        load_scales(s2_raw, w2_scales)
 
-        hz_scales = sb.tile([P, S], U8, name="hz_scales", align_bytes=64)
-        nc.vector.memset(hz_scales[:].bitcast(I32), 0)
-
-        pick_scales = sb.tile([P, S], U8, name="pick_scales", align_bytes=64)
-        nc.vector.tensor_copy(pick_scales[:], x_rows[:].indirect(offs_t[:]))
+        pick_rows = sb.tile([P, S], U8, name="pick_rows")
+        nc.vector.tensor_copy(pick_rows[:], x_rows[:].indirect(offs_t[:]))
+        place_scales(nc.scalar, pick_scales, pick_rows)
         w1_codes = deal(w1_raw, "w1_codes", U16)
         w1_bytes = deal(s1_raw, "w1_bytes", U8)
         pick_codes = sb.tile([P, S], U32, name="pick_codes", align_bytes=64)
@@ -141,13 +149,11 @@ def tile_picked_mixhtrimdot_none_po_kernel(
 
         hz_rows = sb.tile([P, S], U8, name="hz_rows")
         nc.vector.tensor_copy(hz_rows[:], x_rows[:].indirect(hz_t[:]))
-        for r in range(4):
-            first = r if r < 2 else 16 + r
-            nc.sync.dma_start(hz_scales[r:P:32, :].bitcast(I32), hz_rows[first:P:32, :].bitcast(I32))
+        place_scales(nc.sync, hz_scales, hz_rows)
         n5_t = load_list(n5, "n5_t")
         n4_t = load_list(n4, "n4_t")
         n6_t = load_list(n6, "n6_t")
-        hz_codes = sb.tile([P, S], U32, name="hz_codes", tag="s1_raw", align_bytes=64)
+        hz_codes = sb.tile([P, S], U32, name="hz_codes", tag="w1_raw", align_bytes=64)
         nc.vector.tensor_copy(hz_codes[:], x_codes[:].bitcast(U32).indirect(hz_t[:]))
         w3_codes = deal(w3_raw, "w3_codes", U16)
         w3_bytes = deal(s3_raw, "w3_bytes", U8)

from contextlib import ExitStack

import concourse.mybir as mybir

K, T, S, N, H = 512, 2048, 512, 512, 512
FLOPS = 2 * S * (K * H + H * N + K * N)

F32 = mybir.dt.float32
BF16 = mybir.dt.bfloat16
I32 = mybir.dt.int32
U32 = mybir.dt.uint32
U16 = mybir.dt.uint16
U8 = mybir.dt.uint8
FP8X4 = mybir.dt.float8_e4m3fn_x4
FP4X4 = mybir.dt.float4_e2m1fn_x4
ALU = mybir.AluOpType
COPY = mybir.ActivationFunctionType.Copy

P = 128
PACK = 4
QUADS = 4
HALF = S // 2
LAST = PACK - 1
OUT_FACTOR = 0.75

WIDE = 2 * S
STAGES = ((0, HALF), (HALF, HALF + P), (HALF + P, S))
Z_UNITS = (
    [(0, 0, S)]
    + [(t, 0, HALF) for t in range(1, PACK)]
    + [(t, HALF, S) for t in range(1, LAST)]
    + [(LAST, lo, hi) for lo, hi in STAGES[1:]]
)
OUT_UNITS = [(t, 0, S) for t in range(LAST)] + [(LAST, lo, hi) for lo, hi in STAGES]
VECTOR_N3 = 3
FUSED_N4 = (S, HALF, 0, 0)


def tile_picked_mixhtrimdot_none_po_kernel(
    tc, x_words, x_scales, w1_words, w1_scales, gn, w2_words, w2_scales, w3_words, w3_scales,
    offs, n1, n2, n3, hz, n4, n5, n6, out_0, out_1, out_2,
):
    nc = tc.nc
    with ExitStack() as ctx:
        lists = ctx.enter_context(tc.tile_pool(name="lists", bufs=1))
        sb = ctx.enter_context(tc.tile_pool(name="sb", bufs=1))
        psum = ctx.enter_context(tc.psum_pool(name="psum", bufs=1))

        def load_list(src, name):
            offsets = lists.tile([P, S // 16], U16, name=name)
            nc.sync.dma_start(offsets[:], src)
            return offsets

        def load_words(raw, src):
            nc.sync.dma_start(raw[:].bitcast(I32), src[0].bitcast(I32))

        def load_scales(raw, src):
            for q in range(QUADS):
                rows = src[0, 4 * q : 4 * q + 4, :].bitcast(I32)
                nc.sync.dma_start(raw[32 * q : 32 * q + 4, :].bitcast(I32), rows)

        def place_scales(queue, scales, rows):
            for r in range(4):
                queue.dma_start(scales[r:P:32, :].bitcast(I32), rows[8 * r : P : 32, :].bitcast(I32))

        def entries(offsets, lo, hi):
            return offsets[:, lo // 16 : hi // 16]

        def deal(raw, name, dtype):
            dealt = sb.tile(list(raw.shape), U8, name=name, align_bytes=64)
            nc.vector.tensor_copy(
                dealt[:].bitcast(dtype).rearrange("p (t m) -> p t m", t=PACK),
                raw[:].bitcast(dtype).rearrange("p (m t) -> p t m", t=PACK),
            )
            return dealt

        def multiply(acc, w_codes, w_scales, t, codes, scales, start, stop):
            nc.tensor.matmul_mx(
                out=acc,
                lhsT=w_codes[:, 2 * P * t : 2 * P * (t + 1)].bitcast(FP4X4),
                lhsT_scale=w_scales[:, P * t : P * (t + 1)],
                rhs=codes.bitcast(FP8X4),
                rhs_scale=scales,
                start=start,
                stop=stop,
            )

        def woven_view(ap, run):
            return ap.rearrange("p (c i) t -> p c t i", i=run)

        def planar_view(ap, run):
            return ap.rearrange("p t (c i) -> p c t i", i=run)

        def weave(src, name, copy):
            woven = sb.tile([P, src.shape[2], PACK], BF16, name=name, align_bytes=64)
            copy(woven_view(woven[:], 4), planar_view(src, 4))
            return woven

        def quantise(woven, codes, scales):
            nc.vector.quantize_mx(out=codes.bitcast(FP8X4), scales=scales, in_=woven[:].rearrange("p j t -> p (j t)"))

        def fetch_on_scalar(out, window, offsets):
            nc.scalar.activation(out, window[:].indirect(offsets), COPY)

        def planar(name, width=S):
            return sb.tile([P, PACK, width], F32, name=name)

        x_codes = sb.tile([P, T], I32, name="x_codes")
        x_rows = sb.tile([P, T], U8, name="x_rows")
        w1_raw, w2_raw, w3_raw = (
            sb.tile([P, 2 * H], U8, name="w%d_raw" % i, tag="w%d_raw" % i, align_bytes=64) for i in (1, 2, 3)
        )
        s1_raw, s2_raw, s3_raw = (
            sb.tile([P, H], U8, name="s%d_raw" % i, tag="s%d_raw" % i, align_bytes=64) for i in (1, 2, 3)
        )
        pick_scales = sb.tile([P, S], U8, name="pick_scales", align_bytes=64)
        hz_scales = sb.tile([P, S], U8, name="hz_scales", align_bytes=64)
        gain = sb.tile([P, PACK], F32, name="gain")
        for scales in (s1_raw, pick_scales, s3_raw, s2_raw, hz_scales):
            nc.vector.memset(scales[:].bitcast(I32), 0)

        offs_t = load_list(offs, "offs_t")
        x_scale_rows = x_scales[0].bitcast(I32).unsqueeze(1).broadcast_to([P // 8, 8, T // 4])
        nc.scalar.dma_start(x_rows[:].bitcast(I32), x_scale_rows)
        hz_t = load_list(hz, "hz_t")
        load_scales(s1_raw, w1_scales)
        nc.scalar.dma_start(x_codes[:], x_words[0].rearrange("p c r -> p (c r)").bitcast(I32))
        load_words(w1_raw, w1_words)
        n2_t = load_list(n2, "n2_t")
        n3_t = load_list(n3, "n3_t")
        nc.sync.dma_start(gain[:], gn.rearrange("(p t) o -> p (t o)", t=PACK))
        n1_t = load_list(n1, "n1_t")
        load_words(w3_raw, w3_words)
        load_words(w2_raw, w2_words)
        load_scales(s3_raw, w3_scales)
        load_scales(s2_raw, w2_scales)

        pick_rows = sb.tile([P, S], U8, name="pick_rows")
        nc.vector.tensor_copy(pick_rows[:], x_rows[:].indirect(offs_t[:]))
        place_scales(nc.scalar, pick_scales, pick_rows)
        w1_codes = deal(w1_raw, "w1_codes", U16)
        w1_bytes = deal(s1_raw, "w1_bytes", U8)
        pick_codes = sb.tile([P, S], U32, name="pick_codes", align_bytes=64)
        nc.vector.tensor_copy(pick_codes[:], x_codes[:].bitcast(U32).indirect(offs_t[:]))

        y_ps = [psum.tile([P, S], F32, name="y_ps%d" % t, tag="bank%d" % t) for t in range(PACK)]
        for t in range(PACK):
            multiply(y_ps[t][:], w1_codes, w1_bytes, t, pick_codes[:], pick_scales[:], True, True)

        hz_rows = sb.tile([P, S], U8, name="hz_rows")
        nc.vector.tensor_copy(hz_rows[:], x_rows[:].indirect(hz_t[:]))
        place_scales(nc.sync, hz_scales, hz_rows)
        n5_t = load_list(n5, "n5_t")
        n4_t = load_list(n4, "n4_t")
        n6_t = load_list(n6, "n6_t")
        hz_codes = sb.tile([P, S], U32, name="hz_codes", tag="w1_raw", align_bytes=64)
        nc.vector.tensor_copy(hz_codes[:], x_codes[:].bitcast(U32).indirect(hz_t[:]))
        w3_codes = deal(w3_raw, "w3_codes", U16)
        w3_bytes = deal(s3_raw, "w3_bytes", U8)
        w2_codes = deal(w2_raw, "w2_codes", U16)
        w2_bytes = deal(s2_raw, "w2_bytes", U8)

        y = [sb.tile([P, WIDE if t == 0 else S], F32, name="y%d" % t) for t in range(PACK)]
        nc.vector.memset(y[0][:, S:WIDE], 0.0)
        gy = [sb.tile([P, S], F32, name="gy%d" % t) for t in range(PACK)]
        h = [sb.tile([P, WIDE if t < LAST else S], F32, name="h%d" % t) for t in range(PACK)]
        larger = [h[t][:, S:WIDE] for t in range(LAST)] + [sb.tile([P, S], F32, name="larger_last")[:]]
        y_n2, y_n3, rest = planar("y_n2"), planar("y_n3"), planar("rest")
        z_first = planar("z_first", HALF)
        gy_n1 = planar("gy_n1", HALF)
        h_ps = {}

        def round_z(stage):
            lo, hi = STAGES[stage]
            if stage == 0:
                return weave(z_first[:], "z_bf0", nc.vector.tensor_copy)
            woven = sb.tile([P, hi - lo, PACK], BF16, name="z_bf%d" % stage, align_bytes=64)
            looked_up = gy_n1[:, :, lo - HALF : hi - HALF]
            nc.vector.tensor_tensor(
                woven_view(woven[:], 2), planar_view(looked_up, 2), planar_view(rest[:, :, lo:hi], 2), ALU.subtract
            )
            return woven

        def second_product(stage, woven):
            lo, hi = STAGES[stage]
            z_codes = sb.tile([P, hi - lo], U32, name="z_codes%d" % stage, align_bytes=64)
            z_scales = sb.tile([P, hi - lo], U8, name="z_scales%d" % stage, align_bytes=64)
            quantise(woven, z_codes[:], z_scales[:])
            half, start = divmod(lo, HALF)
            if start == 0:
                cols = slice(lo, lo + HALF)
                for t in range(PACK):
                    bank = "bank%d" % (t + PACK * (1 - half))
                    h_ps[half, t] = psum.tile([P, S], F32, name="h_ps%d_%d" % (half, t), tag=bank)[:, 0:HALF]
                    multiply(h_ps[half, t], w3_codes, w3_bytes, t, hz_codes[:, cols], hz_scales[:, cols], True, False)
            for t in range(PACK):
                acc = h_ps[half, t][:, start : start + hi - lo]
                multiply(acc, w2_codes, w2_bytes, t, z_codes[:], z_scales[:], False, hi % HALF == 0)

        rounded = None
        for u, (t, lo, hi) in enumerate(Z_UNITS):
            if lo == 0:
                nc.scalar.activation(y[t][:, 0:S], y_ps[t][:], COPY)
            fetch_on_scalar(y_n2[:, t, lo:hi], y[t], entries(n2_t, lo, hi))
            if u < VECTOR_N3:
                nc.vector.tensor_copy(y_n3[:, t, lo:hi], y[t][:].indirect(entries(n3_t, lo, hi)))
            else:
                fetch_on_scalar(y_n3[:, t, lo:hi], y[t], entries(n3_t, lo, hi))
            if lo == 0:
                nc.vector.tensor_scalar(gy[t][:], y[t][:, 0:S], gain[:, t : t + 1], None, ALU.mult)
            if hi > HALF:
                first = max(lo, HALF)
                fetch_on_scalar(gy_n1[:, t, first - HALF : hi - HALF], gy[t], entries(n1_t, first, hi))
            nc.vector.tensor_tensor(larger[t][:, lo:hi], y_n2[:, t, lo:hi], y_n3[:, t, lo:hi], ALU.max)
            if 0 < u <= PACK:
                before = u - 1
                nc.vector.tensor_tensor(
                    z_first[:, before, :],
                    gy[before][:].indirect(entries(n1_t, 0, HALF)),
                    rest[:, before, 0:HALF],
                    ALU.subtract,
                )
            if rounded:
                second_product(*rounded)
                rounded = None
            nc.vector.scalar_tensor_tensor(
                rest[:, t, lo:hi], larger[t][:, lo:hi], gain[:, t : t + 1], gy[t][:, lo:hi], ALU.mult, ALU.subtract
            )
            if u == PACK:
                rounded = (0, round_z(0))
            if lo > 0 and t == LAST:
                stage = STAGES.index((lo, hi))
                rounded = (stage, round_z(stage))
        second_product(*rounded)

        scaled_h = planar("scaled_h")

        def scale_h(half):
            for t in range(PACK):
                if FUSED_N4[t] > half * HALF:
                    cols = slice(half * HALF, (half + 1) * HALF)
                    nc.scalar.activation(scaled_h[:, t, cols], h_ps[half, t], COPY, scale=OUT_FACTOR)

        for t in range(PACK):
            nc.scalar.activation(h[t][:, 0:HALF], h_ps[0, t], COPY)
        scale_h(0)
        for t in range(PACK):
            if t % 2 == 0:
                nc.vector.tensor_copy(h[t][:, HALF:S], h_ps[1, t])
            else:
                nc.scalar.activation(h[t][:, HALF:S], h_ps[1, t], COPY)
        scale_h(1)

        out_rows = out_0.rearrange("(p t) j -> p t j", t=PACK)
        out_words = out_1[0].rearrange("p c r -> p (c r)").bitcast(I32)
        out_codes = sb.tile([P, S], I32, name="out_codes", align_bytes=64)
        out_scales = sb.tile([P, S], U8, name="out_scales", align_bytes=64)
        h_n4, h_n5, h_n6, own, pair, result = (planar(name) for name in ("h_n4", "h_n5", "h_n6", "own", "pair", "result"))

        def finish(t, lo, hi):
            nc.vector.scalar_tensor_tensor(
                result[:, t, lo:hi], pair[:, t, lo:hi], OUT_FACTOR, own[:, t, lo:hi], ALU.mult, ALU.add
            )
            if hi % HALF == 0:
                stored = slice(lo // HALF * HALF, hi)
                nc.sync.dma_start(out_rows[:, t, stored], result[:, t, stored])
            if t == LAST:
                copy = nc.scalar.copy if lo == 0 else nc.vector.tensor_copy
                woven = weave(result[:, :, lo:hi], "out_bf%d" % lo, copy)
                quantise(woven, out_codes[:, lo:hi], out_scales[:, lo:hi])
                nc.sync.dma_start(out_words[:, lo:hi], out_codes[:, lo:hi])

        for u, (t, lo, hi) in enumerate(OUT_UNITS):
            split = max(lo, FUSED_N4[t])
            fetch_on_scalar(h_n5[:, t, lo:hi], h[t], entries(n5_t, lo, hi))
            if lo < split:
                nc.vector.tensor_tensor(
                    own[:, t, lo:split], h[t][:].indirect(entries(n4_t, lo, split)), scaled_h[:, t, lo:split], ALU.mult
                )
            if split < hi:
                fetch_on_scalar(h_n4[:, t, split:hi], h[t], entries(n4_t, split, hi))
            if lo == 0:
                nc.vector.tensor_tensor(
                    pair[:, t, lo:hi], h[t][:].indirect(entries(n6_t, lo, hi)), h_n5[:, t, lo:hi], ALU.mult
                )
            else:
                fetch_on_scalar(h_n6[:, t, lo:hi], h[t], entries(n6_t, lo, hi))
                nc.vector.tensor_tensor(pair[:, t, lo:hi], h_n6[:, t, lo:hi], h_n5[:, t, lo:hi], ALU.mult)
            if split < hi:
                nc.vector.scalar_tensor_tensor(
                    own[:, t, split:hi], h_n4[:, t, split:hi], OUT_FACTOR, h[t][:, split:hi], ALU.mult, ALU.mult
                )
            if u > 0:
                finish(*OUT_UNITS[u - 1])
        finish(*OUT_UNITS[-1])
        for q in range(QUADS):
            queue = nc.sync if q % 2 else nc.scalar
            queue.dma_start(out_2[0, 4 * q : 4 * q + 4, :].bitcast(I32), out_scales[32 * q : 32 * q + 4, :].bitcast(I32))
